import numpy as np
import ml_dtypes


def mxq(x, axis, fmt="e4m3"):
    dtype, down = {"e4m3": (ml_dtypes.float8_e4m3fn, 7), "e5m2": (ml_dtypes.float8_e5m2, 14)}[fmt]
    v = np.moveaxis(np.asarray(x, np.float32).astype(ml_dtypes.bfloat16).astype(np.float64), axis, -1)
    blocks = v.reshape(v.shape[:-1] + (-1, 32))
    amax = np.abs(blocks).max(-1, keepdims=True)
    byte = np.maximum(np.where(amax > 0, np.frexp(amax)[1] - 1 + 127, 0) - down, 1)
    scale = np.exp2(byte - 127.0)
    codes = (blocks / scale).astype(np.float32).astype(dtype).astype(np.float64)
    return np.moveaxis((codes * scale).reshape(v.shape), -1, axis)


WIDE = False


def mx_kscale(k):
    if not WIDE:
        return np.ones(k)
    levels = np.array([10, -10, 5, -5, 0])
    if k % 512:
        return np.exp2(np.random.permutation(np.resize(levels, k // 32))).repeat(32)
    a = np.empty((k // 512, 16))
    for p in range(k // 512):
        a[p, :8] = np.random.permutation(np.resize(levels, 8))
        for g in range(8):
            far = levels[np.abs(levels - a[p, g]) >= 10]
            a[p, g + 8] = far[np.random.randint(len(far))]
    return np.exp2(a.ravel()).repeat(32)


def f64(x):
    return np.asarray(x).astype(np.float64)


def striped(idx):
    return np.tile(idx.reshape(-1, 16).T, (8, 1)).astype(np.uint16)


def unstriped(offs):
    return offs[:16].T.reshape(-1).astype(np.int64)


def pack_weight(w):
    k, n = w.shape
    w = f64(np.asarray(w, np.float32).astype(ml_dtypes.bfloat16)).reshape(k // 32, 32, n)
    amax = np.abs(w).max(1)
    byte = np.clip(np.where(amax > 0, np.frexp(amax)[1] - 1 + 127 - 7, 1), 1, 254)
    scaled = (w * np.exp2(127.0 - byte)[:, None, :]).reshape(k, n).astype(np.float32)
    words = np.ascontiguousarray(scaled.reshape(k // 512, 128, 4, n).transpose(0, 1, 3, 2)).astype(ml_dtypes.float8_e4m3fn).view(np.uint8)
    return words, np.ascontiguousarray(byte.astype(np.uint8).reshape(k // 512, 16, n))


def unpack_weight(words, scales):
    g, p, n, _ = words.shape
    vals = np.ascontiguousarray(words).view(ml_dtypes.float8_e4m3fn).astype(np.float64) * np.repeat(np.exp2(scales.astype(np.float64) - 127.0), 8, axis=1)[..., None]
    return vals.transpose(0, 1, 3, 2).reshape(g * 512, n)


def relu(v):
    return np.maximum(v, 0.0)


K, T, S, D, N, H, V, U = 512, 2048, 1024, 4, 256, 512, 256, 512


def setup_inputs():
    n = np.random.standard_normal
    s = mx_kscale(K)[:, None]
    u = mx_kscale(H)
    packed_xT = pack_weight(n((K, T)) * s)
    return {
        "x_words": packed_xT[0],
        "x_scales": packed_xT[1],
        "w1": (n((K, H)) / np.sqrt(K) / s).astype(np.float32),
        "w2": (n((K, H)) / np.sqrt(K) / s).astype(np.float32),
        "dst": (np.random.uniform(0.05, 2.0, (H, S))).astype(np.float32),
        "unit": (np.random.uniform(0.6, 1.4, (H, 1)) * u[:, None]).astype(np.float32),
        "w3": (n((H, N)) / np.sqrt(H) / u[:, None]).astype(np.float32),
        "offs": striped(np.random.permutation(T)[:S]),
        "cell": striped(np.random.permutation(np.concatenate([np.arange(V), np.random.randint(0, V, U - V)]))),
    }


def reference(x_words, x_scales, w1, w2, dst, unit, w3, offs, cell):
    ker = (relu(-1.0 * (0.7 * f64(dst)) + 1.0)) ** 2
    xq = unpack_weight(x_words, x_scales)[:, unstriped(offs)]
    y = mxq(f64(w1), 0, "e4m3").T @ xq
    ky = ker * (np.log(np.exp(y) + 1.0))
    alpha = ky.reshape(len(ky), -1, D).sum(axis=2)
    ac = alpha[:, unstriped(cell)]
    ap = ac + 0.2
    ys = mxq(f64(w2), 0, "e4m3").T @ xq
    ks = ker * (np.log(np.exp(ys) + 1.0))
    beta_ = ks.reshape(len(ks), -1, D).sum(axis=2)
    bc = beta_[:, unstriped(cell)]
    bp = bc + 0.2
    mean_ = ap / (ap + bp)
    hid = f64(unit) * mean_
    return mxq(f64(w3), 0, "e4m3").T @ mxq(hid, 0, "e4m3")

@@ -1,0 +1,243 @@
+from contextlib import ExitStack
+
+import concourse.mybir as mybir
+from concourse.masks import make_identity
+
+K, T, S, D, N, H, V, U = 512, 2048, 1024, 4, 256, 512, 256, 512
+FLOPS = 2 * K * H * S * 2 + 2 * H * N * U
+
+F32 = mybir.dt.float32
+BF16 = mybir.dt.bfloat16
+I32 = mybir.dt.int32
+U32 = mybir.dt.uint32
+U16 = mybir.dt.uint16
+U8 = mybir.dt.uint8
+FP8X4 = mybir.dt.float8_e4m3fn_x4
+ALU = mybir.AluOpType
+ACT = mybir.ActivationFunctionType
+
+P = 128
+PACK = 4
+BANK = 512
+HALVES = S // BANK
+QUARTER = 128
+SLOPE = 0.7
+PRIOR = 0.2
+TINY = 2.0 ** -63
+
+
+def tile_picked_ybkiin_mean_p_kernel(tc, x_words, x_scales, w1, w2, dst, unit, w3, offs, cell, out):
+    nc = tc.nc
+    with ExitStack() as ctx:
+        keep = ctx.enter_context(tc.tile_pool(name="keep", bufs=1))
+        psum = ctx.enter_context(tc.psum_pool(name="psum", bufs=1))
+
+        def bank(index, name):
+            return psum.tile([P, BANK], F32, tag="bank%d" % index, name=name)
+
+        offs_sb = keep.tile([P, S // 16], U16, name="offs_sb")
+        nc.sync.dma_start(offs_sb[:], offs)
+
+        table_scales = keep.tile([P, T], U8, name="table_scales", align_bytes=64)
+        nc.gpsimd.memset(table_scales[:].bitcast(I32), 0)
+        for q in range(4):
+            nc.scalar.dma_start(
+                out=table_scales[32 * q : 32 * q + 4, :].bitcast(I32),
+                in_=x_scales[0, 4 * q : 4 * q + 4, :].bitcast(I32),
+            )
+
+        w1_raw = keep.tile([P, PACK, H], F32, name="w1_raw", tag="stage")
+        w_raw = [w1_raw[:]]
+        nc.sync.dma_start(out=w1_raw[:], in_=w1.rearrange("(p j) c -> p j c", j=PACK))
+        table_words = keep.tile([P, T], U32, name="table_words", align_bytes=64)
+        nc.sync.dma_start(
+            out=table_words[:].bitcast(I32),
+            in_=x_words[0].rearrange("p n j -> p (n j)").bitcast(I32),
+        )
+        cell_sb = keep.tile([P, U // 16], U16, name="cell_sb")
+        nc.sync.dma_start(cell_sb[:], cell)
+        unit_sb = keep.tile([P, PACK], F32, name="unit_sb")
+        nc.sync.dma_start(out=unit_sb[:], in_=unit.rearrange("(p t) o -> p (t o)", t=PACK))
+
+        ident = keep.tile([P, P], F32, name="ident")
+        make_identity(nc, ident[:])
+
+        picked_scales = [keep.tile([P, BANK], U8, name="picked_scales%d" % h, align_bytes=64) for h in range(HALVES)]
+        picked_words = [keep.tile([P, BANK], U32, name="picked_words%d" % h, align_bytes=64) for h in range(HALVES)]
+
+        def half_list(h):
+            return offs_sb[:, h * (BANK // 16) : (h + 1) * (BANK // 16)]
+
+        nc.vector.tensor_copy(picked_scales[0][:], table_scales[:].indirect(half_list(0)))
+
+        w_codes = [keep.tile([P, H], U32, name="w_codes%d" % a, align_bytes=64) for a in range(2)]
+        w_scales = [keep.tile([P, H], U8, name="w_scales%d" % a, align_bytes=64) for a in range(2)]
+        w_bf = [keep.tile([P, PACK, P * PACK], BF16, name="w_bf%d" % a, align_bytes=64) for a in range(2)]
+
+        def round_weight(a, m0, m1, copy):
+            src = w_raw[a].rearrange("p j (m t) -> p m j t", t=PACK)
+            dealt = w_bf[a][:].rearrange("p t (m j) -> p m j t", j=PACK)
+            copy(dealt[:, m0:m1], src[:, m0:m1])
+
+        def quantize_weight(a, t0, t1):
+            cols = slice(t0 * P, t1 * P)
+            nc.vector.quantize_mx(
+                out=w_codes[a][:, cols].bitcast(FP8X4),
+                scales=w_scales[a][:, cols],
+                in_=w_bf[a][:, t0:t1, :].rearrange("p t c -> p (t c)"),
+            )
+
+        round_weight(0, 0, P, nc.vector.tensor_copy)
+        quantize_weight(0, 0, PACK)
+        nc.vector.tensor_copy(picked_words[0][:], table_words[:].indirect(half_list(0)))
+        nc.vector.tensor_copy(picked_scales[1][:], table_scales[:].indirect(half_list(1)))
+        nc.vector.tensor_copy(picked_words[1][:], table_words[:].indirect(half_list(1)))
+
+        late = keep.tile([P, PACK * (S + H + N)], F32, name="late", tag="stage")
+        dst_rows = dst.rearrange("(p t) s -> p (t s)", t=PACK)
+        for t in range(PACK):
+            nc.sync.dma_start(out=late[:, t * S : (t + 1) * S], in_=dst_rows[:, t * S : (t + 1) * S])
+        w2_raw = late[:, PACK * S : PACK * (S + H)]
+        nc.sync.dma_start(out=w2_raw, in_=w2.rearrange("(p j) c -> p (j c)", j=PACK))
+        w3_raw = late[:, PACK * (S + H) :]
+        nc.sync.dma_start(out=w3_raw, in_=w3.rearrange("(p t) n -> p (t n)", t=PACK))
+        w_raw.append(w2_raw.rearrange("p (j c) -> p j c", j=PACK))
+
+        work = {}
+        y_bank = {}
+
+        def product_and_sigmoid(a, t, h, index):
+            y = bank(index, "y%d%d%d" % (a, t, h))
+            cols = slice(t * P, (t + 1) * P)
+            nc.tensor.matmul_mx(
+                out=y[:],
+                lhsT=w_codes[a][:, cols].bitcast(FP8X4),
+                lhsT_scale=w_scales[a][:, cols],
+                rhs=picked_words[h][:].bitcast(FP8X4),
+                rhs_scale=picked_scales[h][:],
+                start=True,
+                stop=True,
+            )
+            y_bank[a, t, h] = y[:].rearrange("p (v d) -> p d v", d=D)
+            work[a, t, h] = keep.tile([P, D, P], F32, name="work%d%d%d" % (a, t, h))
+            nc.scalar.activation(work[a, t, h][:], y_bank[a, t, h], ACT.Sigmoid, scale=-1.0)
+
+        def log_of(key):
+            nc.scalar.activation(work[key][:], work[key][:], ACT.Ln, bias=TINY)
+
+        def softplus(key):
+            nc.vector.scalar_tensor_tensor(work[key][:], work[key][:], -1.0, y_bank[key], ALU.mult, ALU.max)
+
+        def weigh(key):
+            a, t, h = key
+            nc.vector.tensor_tensor(work[key][:], work[key][:], ker[t][:, h], ALU.mult)
+
+        first = [(0, t, h) for h in range(HALVES) for t in range(PACK)]
+        second = [(1, t, h) for t in range(PACK) for h in range(HALVES)]
+        for index, key in enumerate(first):
+            product_and_sigmoid(*key, index)
+
+        ker = [keep.tile([P, HALVES, D, P], F32, name="ker%d" % t) for t in range(PACK)]
+
+        def kernel_weights(t, dist):
+            nc.vector.tensor_scalar(
+                ker[t][:].rearrange("p h d v -> p h v d"),
+                dist.rearrange("p (h v d) -> p h v d", h=HALVES, d=D),
+                1.0 / SLOPE,
+                1.0 / SLOPE,
+                ALU.min,
+                ALU.subtract,
+            )
+            for h in range(HALVES):
+                flat = ker[t][:, h].rearrange("p d v -> p (d v)")
+                nc.gpsimd.tensor_tensor(flat, flat, flat, ALU.mult)
+
+        for t in range(PACK):
+            kernel_weights(t, late[:, t * S : (t + 1) * S])
+        round_weight(1, 0, P, nc.vector.tensor_copy)
+        quantize_weight(1, 0, PACK)
+
+        for key in first:
+            log_of(key)
+            softplus(key)
+        for index, key in enumerate(second):
+            product_and_sigmoid(*key, index)
+        for key in first:
+            weigh(key)
+
+        w3_bf = keep.tile([P, N, PACK], BF16, name="w3_bf", align_bytes=64)
+        w3_codes = keep.tile([P, N], U32, name="w3_codes", align_bytes=64)
+        w3_scales = keep.tile([P, N], U8, name="w3_scales", align_bytes=64)
+        nc.vector.tensor_copy(w3_bf[:], w3_raw.rearrange("p (t n) -> p n t", t=PACK))
+        nc.vector.quantize_mx(
+            out=w3_codes[:].bitcast(FP8X4), scales=w3_scales[:], in_=w3_bf[:].rearrange("p n t -> p (n t)")
+        )
+
+        for key in second:
+            log_of(key)
+
+        back = []
+        for t in range(PACK):
+            for h in range(HALVES):
+                softplus((1, t, h))
+                weigh((1, t, h))
+            sums = bank(max(2 * t - 1, 0), "sums%d" % t)
+            for a in range(2):
+                for h in range(HALVES):
+                    cols = slice((a * HALVES + h) * P, (a * HALVES + h + 1) * P)
+                    for d in range(D):
+                        nc.tensor.matmul(
+                            sums[:, cols], work[a, t, h][:, d, :], ident[:],
+                            start=(d == 0), stop=(d == D - 1), is_transpose=True,
+                        )
+            logs = keep.tile([P, 2, V], F32, name="logs%d" % t)
+            nc.scalar.activation(
+                logs[:].rearrange("p a c -> p (a c)"), sums[:], ACT.Ln, bias=PRIOR, scale=SLOPE * SLOPE
+            )
+            odds = keep.tile([P, V], F32, name="odds%d" % t)
+            nc.vector.tensor_tensor(odds[:], logs[:, 0, :], logs[:, 1, :], ALU.subtract)
+            if t == 0:
+                back = [bank(0, "back0"), bank(2, "back1")]
+            for h in range(HALVES):
+                nc.tensor.transpose(back[h][:, t * P : (t + 1) * P], odds[:, h * P : (h + 1) * P], ident[:])
+
+        mean = keep.tile([P, PACK, V], F32, name="mean")
+        for h in range(HALVES):
+            nc.scalar.activation(
+                mean[:, :, h * P : (h + 1) * P], back[h][:].rearrange("p (t v) -> p t v", t=PACK), ACT.Sigmoid
+            )
+        hidden = [keep.tile([P, V], F32, name="hidden%d" % t) for t in range(PACK)]
+        for t in range(PACK):
+            nc.vector.tensor_scalar(hidden[t][:], mean[:, t, :], unit_sb[:, t : t + 1], None, ALU.mult)
+
+        out_rows = out.rearrange("(b p) r -> p b r", p=P)
+        for r in range(U // QUARTER):
+            cols = slice(r * QUARTER, (r + 1) * QUARTER)
+            fetched = keep.tile([P, PACK, QUARTER], BF16, name="fetched%d" % r)
+            for t in range(PACK):
+                window = hidden[t][:].indirect(cell_sb[:, r * (QUARTER // 16) : (r + 1) * (QUARTER // 16)])
+                if t < 2 + r % 2:
+                    nc.scalar.activation(fetched[:, t, :], window, ACT.Copy)
+                else:
+                    nc.vector.tensor_copy(fetched[:, t, :], window)
+            hid = keep.tile([P, QUARTER, PACK], BF16, name="hid%d" % r, align_bytes=64)
+            nc.vector.tensor_copy(hid[:], fetched[:].rearrange("p t r -> p r t"))
+            hid_codes = keep.tile([P, QUARTER], U32, name="hid_codes%d" % r, align_bytes=64)
+            hid_scales = keep.tile([P, QUARTER], U8, name="hid_scales%d" % r, align_bytes=64)
+            nc.vector.quantize_mx(
+                out=hid_codes[:].bitcast(FP8X4), scales=hid_scales[:], in_=hid[:].rearrange("p r t -> p (r t)")
+            )
+            labels = bank(4 + r, "labels%d" % r)
+            for b in range(N // P):
+                nc.tensor.matmul_mx(
+                    out=labels[:, b * QUARTER : (b + 1) * QUARTER],
+                    lhsT=w3_codes[:, b * P : (b + 1) * P].bitcast(FP8X4),
+                    lhsT_scale=w3_scales[:, b * P : (b + 1) * P],
+                    rhs=hid_codes[:].bitcast(FP8X4),
+                    rhs_scale=hid_scales[:],
+                    start=True,
+                    stop=True,
+                )
+            staged = keep.tile([P, N // P, QUARTER], F32, name="staged%d" % r)
+            nc.scalar.copy(staged[:].rearrange("p b r -> p (b r)"), labels[:, 0 : N // P * QUARTER])
+            nc.sync.dma_start(out=out_rows[:, :, cols], in_=staged[:])

@@ -38,12 +38,16 @@ def tile_picked_ybkiin_mean_p_kernel(tc, x_words, x_scales, w1, w2, dst, unit, w
         offs_sb = keep.tile([P, S // 16], U16, name="offs_sb")
         nc.sync.dma_start(offs_sb[:], offs)
 
-        table_scales = keep.tile([P, T], U8, name="table_scales", align_bytes=64)
-        nc.gpsimd.memset(table_scales[:].bitcast(I32), 0)
+        scale_rows = keep.tile([P, T // 4], I32, name="scale_rows")
         for q in range(4):
-            nc.scalar.dma_start(
-                out=table_scales[32 * q : 32 * q + 4, :].bitcast(I32),
-                in_=x_scales[0, 4 * q : 4 * q + 4, :].bitcast(I32),
+            nc.sync.dma_start(
+                out=scale_rows[32 * q : 32 * q + 4, :], in_=x_scales[0, 4 * q : 4 * q + 4, :].bitcast(I32)
+            )
+        table_scales = keep.tile([P, T], U8, name="table_scales", align_bytes=64)
+        nc.vector.memset(table_scales[:].bitcast(I32), 0)
+        for q in range(4):
+            nc.vector.tensor_copy(
+                table_scales[32 * q : 32 * q + 4, :].bitcast(I32), scale_rows[32 * q : 32 * q + 4, :]
             )
 
         w1_raw = keep.tile([P, PACK, H], F32, name="w1_raw", tag="stage")
@@ -87,18 +91,20 @@ def tile_picked_ybkiin_mean_p_kernel(tc, x_words, x_scales, w1, w2, dst, unit, w
                 in_=w_bf[a][:, t0:t1, :].rearrange("p t c -> p (t c)"),
             )
 
-        round_weight(0, 0, P, nc.vector.tensor_copy)
+        round_weight(0, 0, P // 2, nc.scalar.copy)
+        round_weight(0, P // 2, P, nc.vector.tensor_copy)
         quantize_weight(0, 0, PACK)
-        nc.vector.tensor_copy(picked_words[0][:], table_words[:].indirect(half_list(0)))
         nc.vector.tensor_copy(picked_scales[1][:], table_scales[:].indirect(half_list(1)))
+        nc.vector.tensor_copy(picked_words[0][:], table_words[:].indirect(half_list(0)))
         nc.vector.tensor_copy(picked_words[1][:], table_words[:].indirect(half_list(1)))
 
         late = keep.tile([P, PACK * (S + H + N)], F32, name="late", tag="stage")
         dst_rows = dst.rearrange("(p t) s -> p (t s)", t=PACK)
-        for t in range(PACK):
-            nc.sync.dma_start(out=late[:, t * S : (t + 1) * S], in_=dst_rows[:, t * S : (t + 1) * S])
         w2_raw = late[:, PACK * S : PACK * (S + H)]
-        nc.sync.dma_start(out=w2_raw, in_=w2.rearrange("(p j) c -> p (j c)", j=PACK))
+        for t in range(PACK):
+            if t == 2:
+                nc.sync.dma_start(out=w2_raw, in_=w2.rearrange("(p j) c -> p (j c)", j=PACK))
+            nc.sync.dma_start(out=late[:, t * S : (t + 1) * S], in_=dst_rows[:, t * S : (t + 1) * S])
         w3_raw = late[:, PACK * (S + H) :]
         nc.sync.dma_start(out=w3_raw, in_=w3.rearrange("(p t) n -> p (t n)", t=PACK))
         w_raw.append(w2_raw.rearrange("p (j c) -> p j c", j=PACK))
@@ -106,8 +112,9 @@ def tile_picked_ybkiin_mean_p_kernel(tc, x_words, x_scales, w1, w2, dst, unit, w
         work = {}
         y_bank = {}
 
-        def product_and_sigmoid(a, t, h, index):
-            y = bank(index, "y%d%d%d" % (a, t, h))
+        def product(key, index):
+            a, t, h = key
+            y = bank(index, "y%d%d%d" % key)
             cols = slice(t * P, (t + 1) * P)
             nc.tensor.matmul_mx(
                 out=y[:],
@@ -118,9 +125,18 @@ def tile_picked_ybkiin_mean_p_kernel(tc, x_words, x_scales, w1, w2, dst, unit, w
                 start=True,
                 stop=True,
             )
-            y_bank[a, t, h] = y[:].rearrange("p (v d) -> p d v", d=D)
-            work[a, t, h] = keep.tile([P, D, P], F32, name="work%d%d%d" % (a, t, h))
-            nc.scalar.activation(work[a, t, h][:], y_bank[a, t, h], ACT.Sigmoid, scale=-1.0)
+            y_bank[key] = y[:].rearrange("p (v d) -> p d v", d=D)
+
+        def product_and_sigmoid(key, index):
+            product(key, index)
+            work[key] = keep.tile([P, D, P], F32, name="work%d%d%d" % key)
+            nc.scalar.activation(work[key][:], y_bank[key], ACT.Sigmoid, scale=-1.0)
+
+        def group_sums(key, target):
+            for d in range(D):
+                nc.tensor.matmul(
+                    target, work[key][:, d, :], ident[:], start=(d == 0), stop=(d == D - 1), is_transpose=True
+                )
 
         def log_of(key):
             nc.scalar.activation(work[key][:], work[key][:], ACT.Ln, bias=TINY)
@@ -135,9 +151,9 @@ def tile_picked_ybkiin_mean_p_kernel(tc, x_words, x_scales, w1, w2, dst, unit, w
         first = [(0, t, h) for h in range(HALVES) for t in range(PACK)]
         second = [(1, t, h) for t in range(PACK) for h in range(HALVES)]
         for index, key in enumerate(first):
-            product_and_sigmoid(*key, index)
+            product_and_sigmoid(key, index)
 
-        ker = [keep.tile([P, HALVES, D, P], F32, name="ker%d" % t) for t in range(PACK)]
+        ker = [keep.tile([P, HALVES, D, P], F32, name="ker%d" % t, tag="ker%d" % t, align_bytes=64) for t in range(PACK)]
 
         def kernel_weights(t, dist):
             nc.vector.tensor_scalar(
@@ -148,24 +164,65 @@ def tile_picked_ybkiin_mean_p_kernel(tc, x_words, x_scales, w1, w2, dst, unit, w
                 ALU.min,
                 ALU.subtract,
             )
-            for h in range(HALVES):
-                flat = ker[t][:, h].rearrange("p d v -> p (d v)")
-                nc.gpsimd.tensor_tensor(flat, flat, flat, ALU.mult)
 
         for t in range(PACK):
+            if t == 2:
+                round_weight(1, 0, P, nc.vector.tensor_copy)
+                quantize_weight(1, 0, PACK)
             kernel_weights(t, late[:, t * S : (t + 1) * S])
-        round_weight(1, 0, P, nc.vector.tensor_copy)
-        quantize_weight(1, 0, PACK)
 
         for key in first:
             log_of(key)
             softplus(key)
-        for index, key in enumerate(second):
-            product_and_sigmoid(*key, index)
+        for t in range(PACK):
+            flat = ker[t][:].rearrange("p h d v -> p (h d v)")
+            nc.vector.tensor_tensor(flat, flat, flat, ALU.mult)
+        for index, key in enumerate(second[-2:] + second[:-2]):
+            product_and_sigmoid(key, index)
+        sums_for = [bank(h, "sums_for%d" % h) for h in range(HALVES)]
         for key in first:
             weigh(key)
+            group_sums(key, sums_for[key[2]][:, key[1] * P : (key[1] + 1) * P])
 
-        w3_bf = keep.tile([P, N, PACK], BF16, name="w3_bf", align_bytes=64)
+        for key in second[:2]:
+            log_of(key)
+        log_for = keep.tile([P, HALVES, BANK], F32, name="log_for")
+        for h in range(HALVES):
+            nc.scalar.activation(log_for[:, h, :], sums_for[h][:], ACT.Ln, bias=PRIOR, scale=SLOPE * SLOPE)
+        for key in second[2:]:
+            log_of(key)
+        flat = log_for[:].rearrange("p h c -> p (h c)")
+        nc.scalar.activation(flat, flat, ACT.Copy, scale=-1.0)
+
+        log_against = [keep.tile([P, V], F32, name="log_against%d" % t) for t in range(PACK)]
+        back = []
+
+        def turn_back(t):
+            for h in range(HALVES):
+                terms = [log_for[:, h, t * P : (t + 1) * P], log_against[t][:, h * P : (h + 1) * P]]
+                for n, term in enumerate(terms):
+                    nc.tensor.matmul(
+                        back[h][:, t * P : (t + 1) * P], term, ident[:],
+                        start=(n == 0), stop=(n == 1), is_transpose=True,
+                    )
+
+        for t in range(PACK):
+            for h in range(HALVES):
+                softplus((1, t, h))
+                if t == 0:
+                    product((1, PACK - 1, h), 2 + h)
+                weigh((1, t, h))
+            sums = bank(t % 2, "sums_against%d" % t)
+            for h in range(HALVES):
+                group_sums((1, t, h), sums[:, h * P : (h + 1) * P])
+            nc.scalar.activation(log_against[t][:], sums[:, 0:V], ACT.Ln, bias=PRIOR, scale=SLOPE * SLOPE)
+            if t == 1:
+                back.extend([bank(4, "back0"), bank(5, "back1")])
+                turn_back(0)
+            if t >= 1:
+                turn_back(t)
+
+        w3_bf = keep.tile([P, N, PACK], BF16, name="w3_bf", tag="ker3", align_bytes=64)
         w3_codes = keep.tile([P, N], U32, name="w3_codes", align_bytes=64)
         w3_scales = keep.tile([P, N], U8, name="w3_scales", align_bytes=64)
         nc.vector.tensor_copy(w3_bf[:], w3_raw.rearrange("p (t n) -> p n t", t=PACK))
@@ -173,38 +230,10 @@ def tile_picked_ybkiin_mean_p_kernel(tc, x_words, x_scales, w1, w2, dst, unit, w
             out=w3_codes[:].bitcast(FP8X4), scales=w3_scales[:], in_=w3_bf[:].rearrange("p n t -> p (n t)")
         )
 
-        for key in second:
-            log_of(key)
-
-        back = []
-        for t in range(PACK):
-            for h in range(HALVES):
-                softplus((1, t, h))
-                weigh((1, t, h))
-            sums = bank(max(2 * t - 1, 0), "sums%d" % t)
-            for a in range(2):
-                for h in range(HALVES):
-                    cols = slice((a * HALVES + h) * P, (a * HALVES + h + 1) * P)
-                    for d in range(D):
-                        nc.tensor.matmul(
-                            sums[:, cols], work[a, t, h][:, d, :], ident[:],
-                            start=(d == 0), stop=(d == D - 1), is_transpose=True,
-                        )
-            logs = keep.tile([P, 2, V], F32, name="logs%d" % t)
-            nc.scalar.activation(
-                logs[:].rearrange("p a c -> p (a c)"), sums[:], ACT.Ln, bias=PRIOR, scale=SLOPE * SLOPE
-            )
-            odds = keep.tile([P, V], F32, name="odds%d" % t)
-            nc.vector.tensor_tensor(odds[:], logs[:, 0, :], logs[:, 1, :], ALU.subtract)
-            if t == 0:
-                back = [bank(0, "back0"), bank(2, "back1")]
-            for h in range(HALVES):
-                nc.tensor.transpose(back[h][:, t * P : (t + 1) * P], odds[:, h * P : (h + 1) * P], ident[:])
-
         mean = keep.tile([P, PACK, V], F32, name="mean")
         for h in range(HALVES):
             nc.scalar.activation(
-                mean[:, :, h * P : (h + 1) * P], back[h][:].rearrange("p (t v) -> p t v", t=PACK), ACT.Sigmoid
+                mean[:, :, h * P : (h + 1) * P], back[h][:].rearrange("p (t v) -> p t v", t=PACK), ACT.Sigmoid, scale=-1.0
             )
         hidden = [keep.tile([P, V], F32, name="hidden%d" % t) for t in range(PACK)]
         for t in range(PACK):
@@ -227,7 +256,7 @@ def tile_picked_ybkiin_mean_p_kernel(tc, x_words, x_scales, w1, w2, dst, unit, w
             nc.vector.quantize_mx(
                 out=hid_codes[:].bitcast(FP8X4), scales=hid_scales[:], in_=hid[:].rearrange("p r t -> p (r t)")
             )
-            labels = bank(4 + r, "labels%d" % r)
+            labels = bank((0, 2, 3, 6)[r], "labels%d" % r)
             for b in range(N // P):
                 nc.tensor.matmul_mx(
                     out=labels[:, b * QUARTER : (b + 1) * QUARTER],

@@ -50,9 +50,10 @@ def tile_picked_ybkiin_mean_p_kernel(tc, x_words, x_scales, w1, w2, dst, unit, w
                 table_scales[32 * q : 32 * q + 4, :].bitcast(I32), scale_rows[32 * q : 32 * q + 4, :]
             )
 
-        w1_raw = keep.tile([P, PACK, H], F32, name="w1_raw", tag="stage")
-        w_raw = [w1_raw[:]]
-        nc.sync.dma_start(out=w1_raw[:], in_=w1.rearrange("(p j) c -> p j c", j=PACK))
+        w1_rows = w1.rearrange("(p j) c -> p j c", j=PACK)
+        w1_raw = [keep.tile([P, PACK, H // 2], F32, name="w1_raw%d" % n, tag="stage%d" % n) for n in range(2)]
+        for n in range(2):
+            nc.sync.dma_start(out=w1_raw[n][:], in_=w1_rows[:, :, n * (H // 2) : (n + 1) * (H // 2)])
         table_words = keep.tile([P, T], U32, name="table_words", align_bytes=64)
         nc.sync.dma_start(
             out=table_words[:].bitcast(I32),
@@ -78,10 +79,10 @@ def tile_picked_ybkiin_mean_p_kernel(tc, x_words, x_scales, w1, w2, dst, unit, w
         w_scales = [keep.tile([P, H], U8, name="w_scales%d" % a, align_bytes=64) for a in range(2)]
         w_bf = [keep.tile([P, PACK, P * PACK], BF16, name="w_bf%d" % a, align_bytes=64) for a in range(2)]
 
-        def round_weight(a, m0, m1, copy):
-            src = w_raw[a].rearrange("p j (m t) -> p m j t", t=PACK)
-            dealt = w_bf[a][:].rearrange("p t (m j) -> p m j t", j=PACK)
-            copy(dealt[:, m0:m1], src[:, m0:m1])
+        def round_weight(a, raw, m0, copy):
+            src = raw.rearrange("p j (m t) -> p m t j", t=PACK)
+            dealt = w_bf[a][:].rearrange("p t (m j) -> p m t j", j=PACK)
+            copy(dealt[:, m0 : m0 + src.shape[1]], src)
 
         def quantize_weight(a, t0, t1):
             cols = slice(t0 * P, t1 * P)
@@ -91,14 +92,14 @@ def tile_picked_ybkiin_mean_p_kernel(tc, x_words, x_scales, w1, w2, dst, unit, w
                 in_=w_bf[a][:, t0:t1, :].rearrange("p t c -> p (t c)"),
             )
 
-        round_weight(0, 0, P // 2, nc.scalar.copy)
-        round_weight(0, P // 2, P, nc.vector.tensor_copy)
+        for n in range(2):
+            round_weight(0, w1_raw[n][:], n * (P // 2), nc.scalar.copy)
         quantize_weight(0, 0, PACK)
         nc.vector.tensor_copy(picked_scales[1][:], table_scales[:].indirect(half_list(1)))
         nc.vector.tensor_copy(picked_words[0][:], table_words[:].indirect(half_list(0)))
         nc.vector.tensor_copy(picked_words[1][:], table_words[:].indirect(half_list(1)))
 
-        late = keep.tile([P, PACK * (S + H + N)], F32, name="late", tag="stage")
+        late = keep.tile([P, PACK * (S + H + N)], F32, name="late", tag="stage0")
         dst_rows = dst.rearrange("(p t) s -> p (t s)", t=PACK)
         w2_raw = late[:, PACK * S : PACK * (S + H)]
         for t in range(PACK):
@@ -107,10 +108,10 @@ def tile_picked_ybkiin_mean_p_kernel(tc, x_words, x_scales, w1, w2, dst, unit, w
             nc.sync.dma_start(out=late[:, t * S : (t + 1) * S], in_=dst_rows[:, t * S : (t + 1) * S])
         w3_raw = late[:, PACK * (S + H) :]
         nc.sync.dma_start(out=w3_raw, in_=w3.rearrange("(p t) n -> p (t n)", t=PACK))
-        w_raw.append(w2_raw.rearrange("p (j c) -> p j c", j=PACK))
 
         work = {}
         y_bank = {}
+        weighted = {}
 
         def product(key, index):
             a, t, h = key
@@ -125,17 +126,17 @@ def tile_picked_ybkiin_mean_p_kernel(tc, x_words, x_scales, w1, w2, dst, unit, w
                 start=True,
                 stop=True,
             )
-            y_bank[key] = y[:].rearrange("p (v d) -> p d v", d=D)
+            y_bank[key] = y[:]
 
         def product_and_sigmoid(key, index):
             product(key, index)
-            work[key] = keep.tile([P, D, P], F32, name="work%d%d%d" % key)
+            work[key] = keep.tile([P, BANK], F32, name="work%d%d%d" % key)
             nc.scalar.activation(work[key][:], y_bank[key], ACT.Sigmoid, scale=-1.0)
 
         def group_sums(key, target):
             for d in range(D):
                 nc.tensor.matmul(
-                    target, work[key][:, d, :], ident[:], start=(d == 0), stop=(d == D - 1), is_transpose=True
+                    target, weighted[key][:, d // 2, :, d % 2], ident[:], start=(d == 0), stop=(d == D - 1), is_transpose=True
                 )
 
         def log_of(key):
@@ -146,19 +147,25 @@ def tile_picked_ybkiin_mean_p_kernel(tc, x_words, x_scales, w1, w2, dst, unit, w
 
         def weigh(key):
             a, t, h = key
-            nc.vector.tensor_tensor(work[key][:], work[key][:], ker[t][:, h], ALU.mult)
+            weighted[key] = keep.tile([P, 2, P, 2], F32, name="weighted%d%d%d" % key)
+            nc.vector.tensor_tensor(
+                weighted[key][:].rearrange("p u v e -> p v u e"),
+                work[key][:].rearrange("p (v u e) -> p v u e", u=2, e=2),
+                ker[t][:, h * BANK : (h + 1) * BANK].rearrange("p (v u e) -> p v u e", u=2, e=2),
+                ALU.mult,
+            )
 
         first = [(0, t, h) for h in range(HALVES) for t in range(PACK)]
         second = [(1, t, h) for t in range(PACK) for h in range(HALVES)]
         for index, key in enumerate(first):
             product_and_sigmoid(key, index)
 
-        ker = [keep.tile([P, HALVES, D, P], F32, name="ker%d" % t, tag="ker%d" % t, align_bytes=64) for t in range(PACK)]
+        ker = [keep.tile([P, S], F32, name="ker%d" % t, tag="ker%d" % t, align_bytes=64) for t in range(PACK)]
 
         def kernel_weights(t, dist):
             nc.vector.tensor_scalar(
-                ker[t][:].rearrange("p h d v -> p h v d"),
-                dist.rearrange("p (h v d) -> p h v d", h=HALVES, d=D),
+                ker[t][:],
+                dist,
                 1.0 / SLOPE,
                 1.0 / SLOPE,
                 ALU.min,
@@ -167,7 +174,7 @@ def tile_picked_ybkiin_mean_p_kernel(tc, x_words, x_scales, w1, w2, dst, unit, w
 
         for t in range(PACK):
             if t == 2:
-                round_weight(1, 0, P, nc.vector.tensor_copy)
+                round_weight(1, w2_raw.rearrange("p (j c) -> p j c", j=PACK), 0, nc.vector.tensor_copy)
                 quantize_weight(1, 0, PACK)
             kernel_weights(t, late[:, t * S : (t + 1) * S])
 
@@ -175,8 +182,7 @@ def tile_picked_ybkiin_mean_p_kernel(tc, x_words, x_scales, w1, w2, dst, unit, w
             log_of(key)
             softplus(key)
         for t in range(PACK):
-            flat = ker[t][:].rearrange("p h d v -> p (h d v)")
-            nc.vector.tensor_tensor(flat, flat, flat, ALU.mult)
+            nc.vector.tensor_tensor(ker[t][:], ker[t][:], ker[t][:], ALU.mult)
         for index, key in enumerate(second[-2:] + second[:-2]):
             product_and_sigmoid(key, index)
         sums_for = [bank(h, "sums_for%d" % h) for h in range(HALVES)]

@@ -21,6 +21,7 @@ PACK = 4
 BANK = 512
 HALVES = S // BANK
 QUARTER = 128
+ON_GPSIMD = 4
 SLOPE = 0.7
 PRIOR = 0.2
 TINY = 2.0 ** -63
@@ -59,6 +60,8 @@ def tile_picked_ybkiin_mean_p_kernel(tc, x_words, x_scales, w1, w2, dst, unit, w
             out=table_words[:].bitcast(I32),
             in_=x_words[0].rearrange("p n j -> p (n j)").bitcast(I32),
         )
+        w2_raw = keep.tile([P, PACK, H], F32, name="w2_raw")
+        nc.sync.dma_start(out=w2_raw[:], in_=w2.rearrange("(p j) c -> p j c", j=PACK))
         cell_sb = keep.tile([P, U // 16], U16, name="cell_sb")
         nc.sync.dma_start(cell_sb[:], cell)
         unit_sb = keep.tile([P, PACK], F32, name="unit_sb")
@@ -75,8 +78,7 @@ def tile_picked_ybkiin_mean_p_kernel(tc, x_words, x_scales, w1, w2, dst, unit, w
 
         nc.vector.tensor_copy(picked_scales[0][:], table_scales[:].indirect(half_list(0)))
 
-        w_codes = [keep.tile([P, H], U32, name="w_codes%d" % a, align_bytes=64) for a in range(2)]
-        w_scales = [keep.tile([P, H], U8, name="w_scales%d" % a, align_bytes=64) for a in range(2)]
+        w_codes, w_scales = {}, {}
         w_bf = [keep.tile([P, PACK, P * PACK], BF16, name="w_bf%d" % a, align_bytes=64) for a in range(2)]
 
         def round_weight(a, raw, m0, copy):
@@ -85,12 +87,17 @@ def tile_picked_ybkiin_mean_p_kernel(tc, x_words, x_scales, w1, w2, dst, unit, w
             copy(dealt[:, m0 : m0 + src.shape[1]], src)
 
         def quantize_weight(a, t0, t1):
-            cols = slice(t0 * P, t1 * P)
+            name = "%d%d" % (a, t0)
+            codes = keep.tile([P, (t1 - t0) * P], U32, name="w_codes" + name, tag="w_codes" + name, align_bytes=64)
+            scales = keep.tile([P, (t1 - t0) * P], U8, name="w_scales" + name, tag="w_scales" + name, align_bytes=64)
             nc.vector.quantize_mx(
-                out=w_codes[a][:, cols].bitcast(FP8X4),
-                scales=w_scales[a][:, cols],
+                out=codes[:].bitcast(FP8X4),
+                scales=scales[:],
                 in_=w_bf[a][:, t0:t1, :].rearrange("p t c -> p (t c)"),
             )
+            for t in range(t0, t1):
+                w_codes[a, t] = codes[:, (t - t0) * P : (t - t0 + 1) * P]
+                w_scales[a, t] = scales[:, (t - t0) * P : (t - t0 + 1) * P]
 
         for n in range(2):
             round_weight(0, w1_raw[n][:], n * (P // 2), nc.scalar.copy)
@@ -99,136 +106,143 @@ def tile_picked_ybkiin_mean_p_kernel(tc, x_words, x_scales, w1, w2, dst, unit, w
         nc.vector.tensor_copy(picked_words[0][:], table_words[:].indirect(half_list(0)))
         nc.vector.tensor_copy(picked_words[1][:], table_words[:].indirect(half_list(1)))
 
-        late = keep.tile([P, PACK * (S + H + N)], F32, name="late", tag="stage0")
+        late = keep.tile([P, PACK * (S + N)], F32, name="late", tag="stage0")
         dst_rows = dst.rearrange("(p t) s -> p (t s)", t=PACK)
-        w2_raw = late[:, PACK * S : PACK * (S + H)]
         for t in range(PACK):
-            if t == 2:
-                nc.sync.dma_start(out=w2_raw, in_=w2.rearrange("(p j) c -> p (j c)", j=PACK))
             nc.sync.dma_start(out=late[:, t * S : (t + 1) * S], in_=dst_rows[:, t * S : (t + 1) * S])
-        w3_raw = late[:, PACK * (S + H) :]
+        w3_raw = late[:, PACK * S :]
         nc.sync.dma_start(out=w3_raw, in_=w3.rearrange("(p t) n -> p (t n)", t=PACK))
 
         work = {}
         y_bank = {}
-        weighted = {}
 
         def product(key, index):
             a, t, h = key
             y = bank(index, "y%d%d%d" % key)
-            cols = slice(t * P, (t + 1) * P)
             nc.tensor.matmul_mx(
                 out=y[:],
-                lhsT=w_codes[a][:, cols].bitcast(FP8X4),
-                lhsT_scale=w_scales[a][:, cols],
+                lhsT=w_codes[a, t].bitcast(FP8X4),
+                lhsT_scale=w_scales[a, t],
                 rhs=picked_words[h][:].bitcast(FP8X4),
                 rhs_scale=picked_scales[h][:],
                 start=True,
                 stop=True,
             )
-            y_bank[key] = y[:]
+            y_bank[key] = y[:].rearrange("p (v d) -> p d v", d=D)
 
         def product_and_sigmoid(key, index):
             product(key, index)
-            work[key] = keep.tile([P, BANK], F32, name="work%d%d%d" % key)
-            nc.scalar.activation(work[key][:], y_bank[key], ACT.Sigmoid, scale=-1.0)
+            tile = keep.tile([P, D, P], F32, name="work%d%d%d" % key, tag="work%d%d%d" % key)
+            work[key] = tile[:]
+            nc.scalar.activation(work[key], y_bank[key], ACT.Sigmoid, scale=-1.0)
 
         def group_sums(key, target):
             for d in range(D):
                 nc.tensor.matmul(
-                    target, weighted[key][:, d // 2, :, d % 2], ident[:], start=(d == 0), stop=(d == D - 1), is_transpose=True
+                    target, work[key][:, d, :], ident[:], start=(d == 0), stop=(d == D - 1), is_transpose=True
                 )
 
-        def log_of(key):
-            nc.scalar.activation(work[key][:], work[key][:], ACT.Ln, bias=TINY)
+        def log_of(key, target):
+            nc.scalar.activation(target, work[key], ACT.Ln, bias=TINY)
+            work[key] = target
 
         def softplus(key):
-            nc.vector.scalar_tensor_tensor(work[key][:], work[key][:], -1.0, y_bank[key], ALU.mult, ALU.max)
+            nc.vector.scalar_tensor_tensor(work[key], work[key], -1.0, y_bank[key], ALU.mult, ALU.max)
 
-        def weigh(key):
+        def weigh(key, engine, target):
             a, t, h = key
-            weighted[key] = keep.tile([P, 2, P, 2], F32, name="weighted%d%d%d" % key)
-            nc.vector.tensor_tensor(
-                weighted[key][:].rearrange("p u v e -> p v u e"),
-                work[key][:].rearrange("p (v u e) -> p v u e", u=2, e=2),
-                ker[t][:, h * BANK : (h + 1) * BANK].rearrange("p (v u e) -> p v u e", u=2, e=2),
-                ALU.mult,
-            )
+            engine.tensor_tensor(target, work[key], ker[:, h, t], ALU.mult)
+            work[key] = target
 
-        first = [(0, t, h) for h in range(HALVES) for t in range(PACK)]
-        second = [(1, t, h) for t in range(PACK) for h in range(HALVES)]
-        for index, key in enumerate(first):
+        def log_sums(target, sums):
+            nc.scalar.activation(target, sums, ACT.Ln, bias=PRIOR, scale=SLOPE * SLOPE)
+
+        opening = [(0, t, 0) for t in range(PACK)]
+        middle = [(0, t, 1) for t in range(PACK)]
+        early = [(1, t, h) for t in range(2) for h in range(HALVES)]
+        final = [(1, t, h) for t in range(2, PACK) for h in range(HALVES)]
+        for index, key in enumerate(opening + middle):
+            product_and_sigmoid(key, index)
+        round_weight(1, w2_raw[:], 0, nc.vector.tensor_copy)
+        quantize_weight(1, 0, 2)
+        quantize_weight(1, 2, PACK)
+        for index, key in enumerate(early):
             product_and_sigmoid(key, index)
 
-        ker = [keep.tile([P, S], F32, name="ker%d" % t, tag="ker%d" % t, align_bytes=64) for t in range(PACK)]
-
-        def kernel_weights(t, dist):
+        ker = keep.tile([P, HALVES, PACK, D, P], F32, name="ker", tag="ker", align_bytes=64)
+        for t in range(PACK):
             nc.vector.tensor_scalar(
-                ker[t][:],
-                dist,
+                ker[:, :, t].rearrange("p h d v -> p h v d"),
+                late[:, t * S : (t + 1) * S].rearrange("p (h v d) -> p h v d", h=HALVES, d=D),
                 1.0 / SLOPE,
                 1.0 / SLOPE,
                 ALU.min,
                 ALU.subtract,
             )
+        for h in (1, 0):
+            for t in range(0, PACK, 2):
+                pair = ker[:, h, t : t + 2].rearrange("p t d v -> p (t d v)")
+                nc.vector.tensor_tensor(pair, pair, pair, ALU.mult)
 
-        for t in range(PACK):
-            if t == 2:
-                round_weight(1, w2_raw.rearrange("p (j c) -> p j c", j=PACK), 0, nc.vector.tensor_copy)
-                quantize_weight(1, 0, PACK)
-            kernel_weights(t, late[:, t * S : (t + 1) * S])
-
-        for key in first:
-            log_of(key)
+        first = middle + early + opening
+        logs_a = keep.tile([P, ON_GPSIMD, D, P], F32, name="logs_a", tag="w_codes10", align_bytes=64)
+        logs_b = keep.tile([P, len(first) - ON_GPSIMD, D, P], F32, name="logs_b", tag="w_scales10", align_bytes=64)
+        for index, key in enumerate(first):
+            log_of(key, logs_a[:, index] if index < ON_GPSIMD else logs_b[:, index - ON_GPSIMD])
             softplus(key)
-        for t in range(PACK):
-            nc.vector.tensor_tensor(ker[t][:], ker[t][:], ker[t][:], ALU.mult)
-        for index, key in enumerate(second[-2:] + second[:-2]):
+            if index < PACK:
+                product(opening[index], PACK + index)
+            if index < ON_GPSIMD:
+                tile = keep.tile([P, D, P], F32, name="weighed%d" % index)
+                weigh(key, nc.gpsimd, tile[:])
+        for index, key in enumerate(final):
             product_and_sigmoid(key, index)
-        sums_for = [bank(h, "sums_for%d" % h) for h in range(HALVES)]
-        for key in first:
-            weigh(key)
-            group_sums(key, sums_for[key[2]][:, key[1] * P : (key[1] + 1) * P])
 
-        for key in second[:2]:
-            log_of(key)
+        weighed = keep.tile([P, len(first) - ON_GPSIMD, D, P], F32, name="weighed", tag="w_codes10", align_bytes=64)
+        for index, key in enumerate(first[ON_GPSIMD:]):
+            weigh(key, nc.vector, weighed[:, index])
+        sums_for = [bank(4 + h, "sums_for%d" % h) for h in range(HALVES)]
+        sums_early = bank(6, "sums_early")
+        for a, t, h in first:
+            if a == 0:
+                group_sums((a, t, h), sums_for[h][:, t * P : (t + 1) * P])
+            else:
+                group_sums((a, t, h), sums_early[:, t * V + h * P : t * V + (h + 1) * P])
+
+        for key in final:
+            log_of(key, work[key])
         log_for = keep.tile([P, HALVES, BANK], F32, name="log_for")
-        for h in range(HALVES):
-            nc.scalar.activation(log_for[:, h, :], sums_for[h][:], ACT.Ln, bias=PRIOR, scale=SLOPE * SLOPE)
-        for key in second[2:]:
-            log_of(key)
+        for h in (1, 0):
+            log_sums(log_for[:, h, :], sums_for[h][:])
         flat = log_for[:].rearrange("p h c -> p (h c)")
         nc.scalar.activation(flat, flat, ACT.Copy, scale=-1.0)
+        log_against = keep.tile([P, PACK * V], F32, name="log_against")
+        log_sums(log_against[:, 0 : 2 * V], sums_early[:])
 
-        log_against = [keep.tile([P, V], F32, name="log_against%d" % t) for t in range(PACK)]
-        back = []
+        back = [bank(7, "back0"), bank(4, "back1")]
 
         def turn_back(t):
             for h in range(HALVES):
-                terms = [log_for[:, h, t * P : (t + 1) * P], log_against[t][:, h * P : (h + 1) * P]]
+                terms = [log_for[:, h, t * P : (t + 1) * P], log_against[:, t * V + h * P : t * V + (h + 1) * P]]
                 for n, term in enumerate(terms):
                     nc.tensor.matmul(
-                        back[h][:, t * P : (t + 1) * P], term, ident[:],
+                        back[t // 2][:, (t % 2) * V + h * P : (t % 2) * V + (h + 1) * P], term, ident[:],
                         start=(n == 0), stop=(n == 1), is_transpose=True,
                     )
 
-        for t in range(PACK):
+        for t in range(2):
+            turn_back(t)
+        for t in range(2, PACK):
             for h in range(HALVES):
                 softplus((1, t, h))
-                if t == 0:
-                    product((1, PACK - 1, h), 2 + h)
-                weigh((1, t, h))
-            sums = bank(t % 2, "sums_against%d" % t)
+            sums = bank(t - 2, "sums_against%d" % t)
             for h in range(HALVES):
+                weigh((1, t, h), nc.vector, work[1, t, h])
                 group_sums((1, t, h), sums[:, h * P : (h + 1) * P])
-            nc.scalar.activation(log_against[t][:], sums[:, 0:V], ACT.Ln, bias=PRIOR, scale=SLOPE * SLOPE)
-            if t == 1:
-                back.extend([bank(4, "back0"), bank(5, "back1")])
-                turn_back(0)
-            if t >= 1:
-                turn_back(t)
+            log_sums(log_against[:, t * V : (t + 1) * V], sums[:, 0:V])
+            turn_back(t)
 
-        w3_bf = keep.tile([P, N, PACK], BF16, name="w3_bf", tag="ker3", align_bytes=64)
+        w3_bf = keep.tile([P, N, PACK], BF16, name="w3_bf", tag="ker", align_bytes=64)
         w3_codes = keep.tile([P, N], U32, name="w3_codes", align_bytes=64)
         w3_scales = keep.tile([P, N], U8, name="w3_scales", align_bytes=64)
         nc.vector.tensor_copy(w3_bf[:], w3_raw.rearrange("p (t n) -> p n t", t=PACK))
@@ -236,14 +250,14 @@ def tile_picked_ybkiin_mean_p_kernel(tc, x_words, x_scales, w1, w2, dst, unit, w
             out=w3_codes[:].bitcast(FP8X4), scales=w3_scales[:], in_=w3_bf[:].rearrange("p n t -> p (n t)")
         )
 
-        mean = keep.tile([P, PACK, V], F32, name="mean")
-        for h in range(HALVES):
-            nc.scalar.activation(
-                mean[:, :, h * P : (h + 1) * P], back[h][:].rearrange("p (t v) -> p t v", t=PACK), ACT.Sigmoid, scale=-1.0
-            )
         hidden = [keep.tile([P, V], F32, name="hidden%d" % t) for t in range(PACK)]
-        for t in range(PACK):
-            nc.vector.tensor_scalar(hidden[t][:], mean[:, t, :], unit_sb[:, t : t + 1], None, ALU.mult)
+        for pair in range(2):
+            mean = keep.tile([P, 2 * V], F32, name="mean%d" % pair, tag="work13%d" % (1 - pair))
+            nc.scalar.activation(mean[:], back[pair][:], ACT.Sigmoid, scale=-1.0)
+            for t in range(2 * pair, 2 * pair + 2):
+                nc.vector.tensor_scalar(
+                    hidden[t][:], mean[:, (t % 2) * V : (t % 2 + 1) * V], unit_sb[:, t : t + 1], None, ALU.mult
+                )
 
         out_rows = out.rearrange("(b p) r -> p b r", p=P)
         for r in range(U // QUARTER):
@@ -251,7 +265,7 @@ def tile_picked_ybkiin_mean_p_kernel(tc, x_words, x_scales, w1, w2, dst, unit, w
             fetched = keep.tile([P, PACK, QUARTER], BF16, name="fetched%d" % r)
             for t in range(PACK):
                 window = hidden[t][:].indirect(cell_sb[:, r * (QUARTER // 16) : (r + 1) * (QUARTER // 16)])
-                if t < 2 + r % 2:
+                if t > 1 - r % 2:
                     nc.scalar.activation(fetched[:, t, :], window, ACT.Copy)
                 else:
                     nc.vector.tensor_copy(fetched[:, t, :], window)
@@ -262,7 +276,7 @@ def tile_picked_ybkiin_mean_p_kernel(tc, x_words, x_scales, w1, w2, dst, unit, w
             nc.vector.quantize_mx(
                 out=hid_codes[:].bitcast(FP8X4), scales=hid_scales[:], in_=hid[:].rearrange("p r t -> p (r t)")
             )
-            labels = bank((0, 2, 3, 6)[r], "labels%d" % r)
+            labels = bank((2, 3, 5, 6)[r], "labels%d" % r)
             for b in range(N // P):
                 nc.tensor.matmul_mx(
                     out=labels[:, b * QUARTER : (b + 1) * QUARTER],

@@ -18,16 +18,21 @@ ACT = mybir.ActivationFunctionType
 
 P = 128
 PACK = 4
+QUADRANT = 32
+STRIPE = 16
 BANK = 512
 HALVES = S // BANK
 QUARTER = 128
 ON_GPSIMD = 4
+SINGLE_LOGS = 2
 SLOPE = 0.7
 PRIOR = 0.2
 TINY = 2.0 ** -63
 
 
-def tile_picked_ybkiin_mean_p_kernel(tc, x_words, x_scales, w1, w2, dst, unit, w3, offs, cell, out):
+def tile_picked_ybkiin_mean_p_kernel(
+    tc, x_words, x_scales, w1, w2, dst, unit, w3, offs, cell, out
+):
     nc = tc.nc
     with ExitStack() as ctx:
         keep = ctx.enter_context(tc.tile_pool(name="keep", bufs=1))
@@ -36,19 +41,21 @@ def tile_picked_ybkiin_mean_p_kernel(tc, x_words, x_scales, w1, w2, dst, unit, w
         def bank(index, name):
             return psum.tile([P, BANK], F32, tag="bank%d" % index, name=name)
 
-        offs_sb = keep.tile([P, S // 16], U16, name="offs_sb")
+        offs_sb = keep.tile([P, S // STRIPE], U16, name="offs_sb")
         nc.sync.dma_start(offs_sb[:], offs)
 
         scale_rows = keep.tile([P, T // 4], I32, name="scale_rows")
-        for q in range(4):
+        for q in range(P // QUADRANT):
             nc.sync.dma_start(
-                out=scale_rows[32 * q : 32 * q + 4, :], in_=x_scales[0, 4 * q : 4 * q + 4, :].bitcast(I32)
+                out=scale_rows[QUADRANT * q : QUADRANT * q + 4, :],
+                in_=x_scales[0, 4 * q : 4 * q + 4, :].bitcast(I32),
             )
         table_scales = keep.tile([P, T], U8, name="table_scales", align_bytes=64)
         nc.vector.memset(table_scales[:].bitcast(I32), 0)
-        for q in range(4):
+        for q in range(P // QUADRANT):
             nc.vector.tensor_copy(
-                table_scales[32 * q : 32 * q + 4, :].bitcast(I32), scale_rows[32 * q : 32 * q + 4, :]
+                table_scales[QUADRANT * q : QUADRANT * q + 4, :].bitcast(I32),
+                scale_rows[QUADRANT * q : QUADRANT * q + 4, :],
             )
 
         w1_rows = w1.rearrange("(p j) c -> p j c", j=PACK)
@@ -62,7 +69,7 @@ def tile_picked_ybkiin_mean_p_kernel(tc, x_words, x_scales, w1, w2, dst, unit, w
         )
         w2_raw = keep.tile([P, PACK, H], F32, name="w2_raw")
         nc.sync.dma_start(out=w2_raw[:], in_=w2.rearrange("(p j) c -> p j c", j=PACK))
-        cell_sb = keep.tile([P, U // 16], U16, name="cell_sb")
+        cell_sb = keep.tile([P, U // STRIPE], U16, name="cell_sb")
         nc.sync.dma_start(cell_sb[:], cell)
         unit_sb = keep.tile([P, PACK], F32, name="unit_sb")
         nc.sync.dma_start(out=unit_sb[:], in_=unit.rearrange("(p t) o -> p (t o)", t=PACK))
@@ -74,7 +81,7 @@ def tile_picked_ybkiin_mean_p_kernel(tc, x_words, x_scales, w1, w2, dst, unit, w
         picked_words = [keep.tile([P, BANK], U32, name="picked_words%d" % h, align_bytes=64) for h in range(HALVES)]
 
         def half_list(h):
-            return offs_sb[:, h * (BANK // 16) : (h + 1) * (BANK // 16)]
+            return offs_sb[:, h * (BANK // STRIPE) : (h + 1) * (BANK // STRIPE)]
 
         nc.vector.tensor_copy(picked_scales[0][:], table_scales[:].indirect(half_list(0)))
 
@@ -116,9 +123,9 @@ def tile_picked_ybkiin_mean_p_kernel(tc, x_words, x_scales, w1, w2, dst, unit, w
         work = {}
         y_bank = {}
 
-        def product(key, index):
-            a, t, h = key
-            y = bank(index, "y%d%d%d" % key)
+        def product(piece, index):
+            a, t, h = piece
+            y = bank(index, "y%d%d%d" % piece)
             nc.tensor.matmul_mx(
                 out=y[:],
                 lhsT=w_codes[a, t].bitcast(FP8X4),
@@ -128,31 +135,29 @@ def tile_picked_ybkiin_mean_p_kernel(tc, x_words, x_scales, w1, w2, dst, unit, w
                 start=True,
                 stop=True,
             )
-            y_bank[key] = y[:].rearrange("p (v d) -> p d v", d=D)
+            y_bank[piece] = y[:].rearrange("p (v d) -> p d v", d=D)
 
-        def product_and_sigmoid(key, index):
-            product(key, index)
-            tile = keep.tile([P, D, P], F32, name="work%d%d%d" % key, tag="work%d%d%d" % key)
-            work[key] = tile[:]
-            nc.scalar.activation(work[key], y_bank[key], ACT.Sigmoid, scale=-1.0)
+        def product_and_sigmoid(piece, index, target):
+            product(piece, index)
+            nc.scalar.activation(target, y_bank[piece], ACT.Sigmoid, scale=-1.0)
+            work[piece] = target
 
-        def group_sums(key, target):
+        def log_sigmoid(target, source):
+            nc.scalar.activation(target, source, ACT.Ln, bias=TINY)
+
+        def softplus(piece):
+            nc.vector.scalar_tensor_tensor(work[piece], work[piece], -1.0, y_bank[piece], ALU.mult, ALU.max)
+
+        def weigh(piece, engine, target):
+            a, t, h = piece
+            engine.tensor_tensor(target, work[piece], ker[:, t, h], ALU.mult)
+            work[piece] = target
+
+        def group_sums(piece, target):
             for d in range(D):
                 nc.tensor.matmul(
-                    target, work[key][:, d, :], ident[:], start=(d == 0), stop=(d == D - 1), is_transpose=True
+                    target, work[piece][:, d, :], ident[:], start=(d == 0), stop=(d == D - 1), is_transpose=True
                 )
-
-        def log_of(key, target):
-            nc.scalar.activation(target, work[key], ACT.Ln, bias=TINY)
-            work[key] = target
-
-        def softplus(key):
-            nc.vector.scalar_tensor_tensor(work[key], work[key], -1.0, y_bank[key], ALU.mult, ALU.max)
-
-        def weigh(key, engine, target):
-            a, t, h = key
-            engine.tensor_tensor(target, work[key], ker[:, h, t], ALU.mult)
-            work[key] = target
 
         def log_sums(target, sums):
             nc.scalar.activation(target, sums, ACT.Ln, bias=PRIOR, scale=SLOPE * SLOPE)
@@ -161,46 +166,55 @@ def tile_picked_ybkiin_mean_p_kernel(tc, x_words, x_scales, w1, w2, dst, unit, w
         middle = [(0, t, 1) for t in range(PACK)]
         early = [(1, t, h) for t in range(2) for h in range(HALVES)]
         final = [(1, t, h) for t in range(2, PACK) for h in range(HALVES)]
-        for index, key in enumerate(opening + middle):
-            product_and_sigmoid(key, index)
+        first = middle + early + opening
+
+        sigmoids = keep.tile([P, len(first), D, P], F32, name="sigmoids")
+        for index, piece in enumerate(opening + middle):
+            product_and_sigmoid(piece, index, sigmoids[:, first.index(piece)])
         round_weight(1, w2_raw[:], 0, nc.vector.tensor_copy)
         quantize_weight(1, 0, 2)
         quantize_weight(1, 2, PACK)
-        for index, key in enumerate(early):
-            product_and_sigmoid(key, index)
+        for index, piece in enumerate(early):
+            product_and_sigmoid(piece, index, sigmoids[:, first.index(piece)])
 
-        ker = keep.tile([P, HALVES, PACK, D, P], F32, name="ker", tag="ker", align_bytes=64)
+        ker = keep.tile([P, PACK, HALVES, D, P], F32, name="ker", tag="ker", align_bytes=64)
         for t in range(PACK):
             nc.vector.tensor_scalar(
-                ker[:, :, t].rearrange("p h d v -> p h v d"),
+                ker[:, t].rearrange("p h d v -> p h v d"),
                 late[:, t * S : (t + 1) * S].rearrange("p (h v d) -> p h v d", h=HALVES, d=D),
                 1.0 / SLOPE,
                 1.0 / SLOPE,
                 ALU.min,
                 ALU.subtract,
             )
-        for h in (1, 0):
-            for t in range(0, PACK, 2):
-                pair = ker[:, h, t : t + 2].rearrange("p t d v -> p (t d v)")
-                nc.vector.tensor_tensor(pair, pair, pair, ALU.mult)
+            row = ker[:, t].rearrange("p h d v -> p (h d v)")
+            nc.vector.tensor_tensor(row, row, row, ALU.mult)
 
-        first = middle + early + opening
         logs_a = keep.tile([P, ON_GPSIMD, D, P], F32, name="logs_a", tag="w_codes10", align_bytes=64)
         logs_b = keep.tile([P, len(first) - ON_GPSIMD, D, P], F32, name="logs_b", tag="w_scales10", align_bytes=64)
-        for index, key in enumerate(first):
-            log_of(key, logs_a[:, index] if index < ON_GPSIMD else logs_b[:, index - ON_GPSIMD])
-            softplus(key)
-            if index < PACK:
-                product(opening[index], PACK + index)
+        weighed_a = keep.tile([P, ON_GPSIMD, D, P], F32, name="weighed_a")
+        for index, piece in enumerate(first):
+            logs, place = (logs_a, index) if index < ON_GPSIMD else (logs_b, index - ON_GPSIMD)
+            if index < SINGLE_LOGS:
+                log_sigmoid(logs[:, place], sigmoids[:, index])
+            elif index % 2 == 0:
+                log_sigmoid(logs[:, place : place + 2], sigmoids[:, index : index + 2])
+            work[piece] = logs[:, place]
+            softplus(piece)
+            if index < len(opening):
+                product(opening[index], len(opening) + index)
             if index < ON_GPSIMD:
-                tile = keep.tile([P, D, P], F32, name="weighed%d" % index)
-                weigh(key, nc.gpsimd, tile[:])
-        for index, key in enumerate(final):
-            product_and_sigmoid(key, index)
+                weigh(piece, nc.gpsimd, weighed_a[:, index])
 
-        weighed = keep.tile([P, len(first) - ON_GPSIMD, D, P], F32, name="weighed", tag="w_codes10", align_bytes=64)
-        for index, key in enumerate(first[ON_GPSIMD:]):
-            weigh(key, nc.vector, weighed[:, index])
+        for index, piece in enumerate(final):
+            tile = keep.tile([P, D, P], F32, name="work%d%d%d" % piece, tag="work%d%d%d" % piece)
+            product_and_sigmoid(piece, index, tile[:])
+
+        weighed_b = keep.tile(
+            [P, len(first) - ON_GPSIMD, D, P], F32, name="weighed_b", tag="w_codes10", align_bytes=64
+        )
+        for index, piece in enumerate(first[ON_GPSIMD:]):
+            weigh(piece, nc.vector, weighed_b[:, index])
         sums_for = [bank(4 + h, "sums_for%d" % h) for h in range(HALVES)]
         sums_early = bank(6, "sums_early")
         for a, t, h in first:
@@ -209,8 +223,8 @@ def tile_picked_ybkiin_mean_p_kernel(tc, x_words, x_scales, w1, w2, dst, unit, w
             else:
                 group_sums((a, t, h), sums_early[:, t * V + h * P : t * V + (h + 1) * P])
 
-        for key in final:
-            log_of(key, work[key])
+        for piece in final:
+            log_sigmoid(work[piece], work[piece])
         log_for = keep.tile([P, HALVES, BANK], F32, name="log_for")
         for h in (1, 0):
             log_sums(log_for[:, h, :], sums_for[h][:])
@@ -226,18 +240,28 @@ def tile_picked_ybkiin_mean_p_kernel(tc, x_words, x_scales, w1, w2, dst, unit, w
                 terms = [log_for[:, h, t * P : (t + 1) * P], log_against[:, t * V + h * P : t * V + (h + 1) * P]]
                 for n, term in enumerate(terms):
                     nc.tensor.matmul(
-                        back[t // 2][:, (t % 2) * V + h * P : (t % 2) * V + (h + 1) * P], term, ident[:],
-                        start=(n == 0), stop=(n == 1), is_transpose=True,
+                        back[t // 2][:, (t % 2) * V + h * P : (t % 2) * V + (h + 1) * P],
+                        term,
+                        ident[:],
+                        start=(n == 0),
+                        stop=(n == 1),
+                        is_transpose=True,
                     )
 
         for t in range(2):
             turn_back(t)
+
+        for piece in final:
+            softplus(piece)
+        handover = "work%d%d%d" % final[0]
+        weighed_c = keep.tile([P, D, P], F32, name="weighed_c")
+        weigh(final[0], nc.gpsimd, weighed_c[:])
+        weighed_d = keep.tile([P, len(final) - 1, D, P], F32, name="weighed_d", tag=handover)
+        for index, piece in enumerate(final[1:]):
+            weigh(piece, nc.vector, weighed_d[:, index])
         for t in range(2, PACK):
-            for h in range(HALVES):
-                softplus((1, t, h))
             sums = bank(t - 2, "sums_against%d" % t)
             for h in range(HALVES):
-                weigh((1, t, h), nc.vector, work[1, t, h])
                 group_sums((1, t, h), sums[:, h * P : (h + 1) * P])
             log_sums(log_against[:, t * V : (t + 1) * V], sums[:, 0:V])
             turn_back(t)
@@ -251,8 +275,8 @@ def tile_picked_ybkiin_mean_p_kernel(tc, x_words, x_scales, w1, w2, dst, unit, w
         )
 
         hidden = [keep.tile([P, V], F32, name="hidden%d" % t) for t in range(PACK)]
-        for pair in range(2):
-            mean = keep.tile([P, 2 * V], F32, name="mean%d" % pair, tag="work13%d" % (1 - pair))
+        for pair, tag in enumerate((handover, "mean1")):
+            mean = keep.tile([P, 2 * V], F32, name="mean%d" % pair, tag=tag)
             nc.scalar.activation(mean[:], back[pair][:], ACT.Sigmoid, scale=-1.0)
             for t in range(2 * pair, 2 * pair + 2):
                 nc.vector.tensor_scalar(
@@ -260,15 +284,16 @@ def tile_picked_ybkiin_mean_p_kernel(tc, x_words, x_scales, w1, w2, dst, unit, w
                 )
 
         out_rows = out.rearrange("(b p) r -> p b r", p=P)
+        label_banks = (2, 3, 5, 6)
         for r in range(U // QUARTER):
-            cols = slice(r * QUARTER, (r + 1) * QUARTER)
             fetched = keep.tile([P, PACK, QUARTER], BF16, name="fetched%d" % r)
+            on_vector = 2 - r % 2
             for t in range(PACK):
-                window = hidden[t][:].indirect(cell_sb[:, r * (QUARTER // 16) : (r + 1) * (QUARTER // 16)])
-                if t > 1 - r % 2:
-                    nc.scalar.activation(fetched[:, t, :], window, ACT.Copy)
-                else:
+                window = hidden[t][:].indirect(cell_sb[:, r * (QUARTER // STRIPE) : (r + 1) * (QUARTER // STRIPE)])
+                if t < on_vector:
                     nc.vector.tensor_copy(fetched[:, t, :], window)
+                else:
+                    nc.scalar.activation(fetched[:, t, :], window, ACT.Copy)
             hid = keep.tile([P, QUARTER, PACK], BF16, name="hid%d" % r, align_bytes=64)
             nc.vector.tensor_copy(hid[:], fetched[:].rearrange("p t r -> p r t"))
             hid_codes = keep.tile([P, QUARTER], U32, name="hid_codes%d" % r, align_bytes=64)
@@ -276,7 +301,7 @@ def tile_picked_ybkiin_mean_p_kernel(tc, x_words, x_scales, w1, w2, dst, unit, w
             nc.vector.quantize_mx(
                 out=hid_codes[:].bitcast(FP8X4), scales=hid_scales[:], in_=hid[:].rearrange("p r t -> p (r t)")
             )
-            labels = bank((2, 3, 5, 6)[r], "labels%d" % r)
+            labels = bank(label_banks[r], "labels%d" % r)
             for b in range(N // P):
                 nc.tensor.matmul_mx(
                     out=labels[:, b * QUARTER : (b + 1) * QUARTER],
@@ -289,4 +314,4 @@ def tile_picked_ybkiin_mean_p_kernel(tc, x_words, x_scales, w1, w2, dst, unit, w
                 )
             staged = keep.tile([P, N // P, QUARTER], F32, name="staged%d" % r)
             nc.scalar.copy(staged[:].rearrange("p b r -> p (b r)"), labels[:, 0 : N // P * QUARTER])
-            nc.sync.dma_start(out=out_rows[:, :, cols], in_=staged[:])
+            nc.sync.dma_start(out=out_rows[:, :, r * QUARTER : (r + 1) * QUARTER], in_=staged[:])

from contextlib import ExitStack

import concourse.mybir as mybir
from concourse.masks import make_identity

K, T, S, D, N, H, V, U = 512, 2048, 1024, 4, 256, 512, 256, 512
FLOPS = 2 * K * H * S * 2 + 2 * H * N * U

F32 = mybir.dt.float32
BF16 = mybir.dt.bfloat16
I32 = mybir.dt.int32
U32 = mybir.dt.uint32
U16 = mybir.dt.uint16
U8 = mybir.dt.uint8
FP8X4 = mybir.dt.float8_e4m3fn_x4
ALU = mybir.AluOpType
ACT = mybir.ActivationFunctionType

P = 128
PACK = 4
QUADRANT = 32
STRIPE = 16
BANK = 512
HALVES = S // BANK
QUARTER = 128
ON_GPSIMD = 4
SINGLE_LOGS = 2
SLOPE = 0.7
PRIOR = 0.2
TINY = 2.0 ** -63


def tile_picked_ybkiin_mean_p_kernel(
    tc, x_words, x_scales, w1, w2, dst, unit, w3, offs, cell, out
):
    nc = tc.nc
    with ExitStack() as ctx:
        keep = ctx.enter_context(tc.tile_pool(name="keep", bufs=1))
        psum = ctx.enter_context(tc.psum_pool(name="psum", bufs=1))

        def bank(index, name):
            return psum.tile([P, BANK], F32, tag="bank%d" % index, name=name)

        offs_sb = keep.tile([P, S // STRIPE], U16, name="offs_sb")
        nc.sync.dma_start(offs_sb[:], offs)

        scale_rows = keep.tile([P, T // 4], I32, name="scale_rows")
        for q in range(P // QUADRANT):
            nc.sync.dma_start(
                out=scale_rows[QUADRANT * q : QUADRANT * q + 4, :],
                in_=x_scales[0, 4 * q : 4 * q + 4, :].bitcast(I32),
            )
        table_scales = keep.tile([P, T], U8, name="table_scales", align_bytes=64)
        nc.vector.memset(table_scales[:].bitcast(I32), 0)
        for q in range(P // QUADRANT):
            nc.vector.tensor_copy(
                table_scales[QUADRANT * q : QUADRANT * q + 4, :].bitcast(I32),
                scale_rows[QUADRANT * q : QUADRANT * q + 4, :],
            )

        w1_rows = w1.rearrange("(p j) c -> p j c", j=PACK)
        w1_raw = [keep.tile([P, PACK, H // 2], F32, name="w1_raw%d" % n, tag="stage%d" % n) for n in range(2)]
        for n in range(2):
            nc.sync.dma_start(out=w1_raw[n][:], in_=w1_rows[:, :, n * (H // 2) : (n + 1) * (H // 2)])
        table_words = keep.tile([P, T], U32, name="table_words", align_bytes=64)
        nc.sync.dma_start(
            out=table_words[:].bitcast(I32),
            in_=x_words[0].rearrange("p n j -> p (n j)").bitcast(I32),
        )
        w2_raw = keep.tile([P, PACK, H], F32, name="w2_raw")
        nc.sync.dma_start(out=w2_raw[:], in_=w2.rearrange("(p j) c -> p j c", j=PACK))
        cell_sb = keep.tile([P, U // STRIPE], U16, name="cell_sb")
        nc.sync.dma_start(cell_sb[:], cell)
        unit_sb = keep.tile([P, PACK], F32, name="unit_sb")
        nc.sync.dma_start(out=unit_sb[:], in_=unit.rearrange("(p t) o -> p (t o)", t=PACK))

        ident = keep.tile([P, P], F32, name="ident")
        make_identity(nc, ident[:])

        picked_scales = [keep.tile([P, BANK], U8, name="picked_scales%d" % h, align_bytes=64) for h in range(HALVES)]
        picked_words = [keep.tile([P, BANK], U32, name="picked_words%d" % h, align_bytes=64) for h in range(HALVES)]

        def half_list(h):
            return offs_sb[:, h * (BANK // STRIPE) : (h + 1) * (BANK // STRIPE)]

        nc.vector.tensor_copy(picked_scales[0][:], table_scales[:].indirect(half_list(0)))

        w_codes, w_scales = {}, {}
        w_bf = [keep.tile([P, PACK, P * PACK], BF16, name="w_bf%d" % a, align_bytes=64) for a in range(2)]

        def round_weight(a, raw, m0, copy):
            src = raw.rearrange("p j (m t) -> p m t j", t=PACK)
            dealt = w_bf[a][:].rearrange("p t (m j) -> p m t j", j=PACK)
            copy(dealt[:, m0 : m0 + src.shape[1]], src)

        def quantize_weight(a, t0, t1):
            name = "%d%d" % (a, t0)
            codes = keep.tile([P, (t1 - t0) * P], U32, name="w_codes" + name, tag="w_codes" + name, align_bytes=64)
            scales = keep.tile([P, (t1 - t0) * P], U8, name="w_scales" + name, tag="w_scales" + name, align_bytes=64)
            nc.vector.quantize_mx(
                out=codes[:].bitcast(FP8X4),
                scales=scales[:],
                in_=w_bf[a][:, t0:t1, :].rearrange("p t c -> p (t c)"),
            )
            for t in range(t0, t1):
                w_codes[a, t] = codes[:, (t - t0) * P : (t - t0 + 1) * P]
                w_scales[a, t] = scales[:, (t - t0) * P : (t - t0 + 1) * P]

        for n in range(2):
            round_weight(0, w1_raw[n][:], n * (P // 2), nc.scalar.copy)
        quantize_weight(0, 0, PACK)
        nc.vector.tensor_copy(picked_scales[1][:], table_scales[:].indirect(half_list(1)))
        nc.vector.tensor_copy(picked_words[0][:], table_words[:].indirect(half_list(0)))
        nc.vector.tensor_copy(picked_words[1][:], table_words[:].indirect(half_list(1)))

        late = keep.tile([P, PACK * (S + N)], F32, name="late", tag="stage0")
        dst_rows = dst.rearrange("(p t) s -> p (t s)", t=PACK)
        for t in range(PACK):
            nc.sync.dma_start(out=late[:, t * S : (t + 1) * S], in_=dst_rows[:, t * S : (t + 1) * S])
        w3_raw = late[:, PACK * S :]
        nc.sync.dma_start(out=w3_raw, in_=w3.rearrange("(p t) n -> p (t n)", t=PACK))

        work = {}
        y_bank = {}

        def product(piece, index):
            a, t, h = piece
            y = bank(index, "y%d%d%d" % piece)
            nc.tensor.matmul_mx(
                out=y[:],
                lhsT=w_codes[a, t].bitcast(FP8X4),
                lhsT_scale=w_scales[a, t],
                rhs=picked_words[h][:].bitcast(FP8X4),
                rhs_scale=picked_scales[h][:],
                start=True,
                stop=True,
            )
            y_bank[piece] = y[:].rearrange("p (v d) -> p d v", d=D)

        def product_and_sigmoid(piece, index, target):
            product(piece, index)
            nc.scalar.activation(target, y_bank[piece], ACT.Sigmoid, scale=-1.0)
            work[piece] = target

        def log_sigmoid(target, source):
            nc.scalar.activation(target, source, ACT.Ln, bias=TINY)

        def softplus(piece):
            nc.vector.scalar_tensor_tensor(work[piece], work[piece], -1.0, y_bank[piece], ALU.mult, ALU.max)

        def weigh(piece, engine, target):
            a, t, h = piece
            engine.tensor_tensor(target, work[piece], ker[:, t, h], ALU.mult)
            work[piece] = target

        def group_sums(piece, target):
            for d in range(D):
                nc.tensor.matmul(
                    target, work[piece][:, d, :], ident[:], start=(d == 0), stop=(d == D - 1), is_transpose=True
                )

        def log_sums(target, sums):
            nc.scalar.activation(target, sums, ACT.Ln, bias=PRIOR, scale=SLOPE * SLOPE)

        opening = [(0, t, 0) for t in range(PACK)]
        middle = [(0, t, 1) for t in range(PACK)]
        early = [(1, t, h) for t in range(2) for h in range(HALVES)]
        final = [(1, t, h) for t in range(2, PACK) for h in range(HALVES)]
        first = middle + early + opening

        sigmoids = keep.tile([P, len(first), D, P], F32, name="sigmoids")
        for index, piece in enumerate(opening + middle):
            product_and_sigmoid(piece, index, sigmoids[:, first.index(piece)])
        round_weight(1, w2_raw[:], 0, nc.vector.tensor_copy)
        quantize_weight(1, 0, 2)
        quantize_weight(1, 2, PACK)
        for index, piece in enumerate(early):
            product_and_sigmoid(piece, index, sigmoids[:, first.index(piece)])

        ker = keep.tile([P, PACK, HALVES, D, P], F32, name="ker", tag="ker", align_bytes=64)
        for t in range(PACK):
            nc.vector.tensor_scalar(
                ker[:, t].rearrange("p h d v -> p h v d"),
                late[:, t * S : (t + 1) * S].rearrange("p (h v d) -> p h v d", h=HALVES, d=D),
                1.0 / SLOPE,
                1.0 / SLOPE,
                ALU.min,
                ALU.subtract,
            )
            row = ker[:, t].rearrange("p h d v -> p (h d v)")
            nc.vector.tensor_tensor(row, row, row, ALU.mult)

        logs_a = keep.tile([P, ON_GPSIMD, D, P], F32, name="logs_a", tag="w_codes10", align_bytes=64)
        logs_b = keep.tile([P, len(first) - ON_GPSIMD, D, P], F32, name="logs_b", tag="w_scales10", align_bytes=64)
        weighed_a = keep.tile([P, ON_GPSIMD, D, P], F32, name="weighed_a")
        for index, piece in enumerate(first):
            logs, place = (logs_a, index) if index < ON_GPSIMD else (logs_b, index - ON_GPSIMD)
            if index < SINGLE_LOGS:
                log_sigmoid(logs[:, place], sigmoids[:, index])
            elif index % 2 == 0:
                log_sigmoid(logs[:, place : place + 2], sigmoids[:, index : index + 2])
            work[piece] = logs[:, place]
            softplus(piece)
            if index < len(opening):
                product(opening[index], len(opening) + index)
            if index < ON_GPSIMD:
                weigh(piece, nc.gpsimd, weighed_a[:, index])

        for index, piece in enumerate(final):
            tile = keep.tile([P, D, P], F32, name="work%d%d%d" % piece, tag="work%d%d%d" % piece)
            product_and_sigmoid(piece, index, tile[:])

        weighed_b = keep.tile(
            [P, len(first) - ON_GPSIMD, D, P], F32, name="weighed_b", tag="w_codes10", align_bytes=64
        )
        for index, piece in enumerate(first[ON_GPSIMD:]):
            weigh(piece, nc.vector, weighed_b[:, index])
        sums_for = [bank(4 + h, "sums_for%d" % h) for h in range(HALVES)]
        sums_early = bank(6, "sums_early")
        for a, t, h in first:
            if a == 0:
                group_sums((a, t, h), sums_for[h][:, t * P : (t + 1) * P])
            else:
                group_sums((a, t, h), sums_early[:, t * V + h * P : t * V + (h + 1) * P])

        for piece in final:
            log_sigmoid(work[piece], work[piece])
        log_for = keep.tile([P, HALVES, BANK], F32, name="log_for")
        for h in (1, 0):
            log_sums(log_for[:, h, :], sums_for[h][:])
        flat = log_for[:].rearrange("p h c -> p (h c)")
        nc.scalar.activation(flat, flat, ACT.Copy, scale=-1.0)
        log_against = keep.tile([P, PACK * V], F32, name="log_against")
        log_sums(log_against[:, 0 : 2 * V], sums_early[:])

        back = [bank(7, "back0"), bank(4, "back1")]

        def turn_back(t):
            for h in range(HALVES):
                terms = [log_for[:, h, t * P : (t + 1) * P], log_against[:, t * V + h * P : t * V + (h + 1) * P]]
                for n, term in enumerate(terms):
                    nc.tensor.matmul(
                        back[t // 2][:, (t % 2) * V + h * P : (t % 2) * V + (h + 1) * P],
                        term,
                        ident[:],
                        start=(n == 0),
                        stop=(n == 1),
                        is_transpose=True,
                    )

        for t in range(2):
            turn_back(t)

        for piece in final:
            softplus(piece)
        handover = "work%d%d%d" % final[0]
        weighed_c = keep.tile([P, D, P], F32, name="weighed_c")
        weigh(final[0], nc.gpsimd, weighed_c[:])
        weighed_d = keep.tile([P, len(final) - 1, D, P], F32, name="weighed_d", tag=handover)
        for index, piece in enumerate(final[1:]):
            weigh(piece, nc.vector, weighed_d[:, index])
        for t in range(2, PACK):
            sums = bank(t - 2, "sums_against%d" % t)
            for h in range(HALVES):
                group_sums((1, t, h), sums[:, h * P : (h + 1) * P])
            log_sums(log_against[:, t * V : (t + 1) * V], sums[:, 0:V])
            turn_back(t)

        w3_bf = keep.tile([P, N, PACK], BF16, name="w3_bf", tag="ker", align_bytes=64)
        w3_codes = keep.tile([P, N], U32, name="w3_codes", align_bytes=64)
        w3_scales = keep.tile([P, N], U8, name="w3_scales", align_bytes=64)
        nc.vector.tensor_copy(w3_bf[:], w3_raw.rearrange("p (t n) -> p n t", t=PACK))
        nc.vector.quantize_mx(
            out=w3_codes[:].bitcast(FP8X4), scales=w3_scales[:], in_=w3_bf[:].rearrange("p n t -> p (n t)")
        )

        hidden = [keep.tile([P, V], F32, name="hidden%d" % t) for t in range(PACK)]
        for pair, tag in enumerate((handover, "mean1")):
            mean = keep.tile([P, 2 * V], F32, name="mean%d" % pair, tag=tag)
            nc.scalar.activation(mean[:], back[pair][:], ACT.Sigmoid, scale=-1.0)
            for t in range(2 * pair, 2 * pair + 2):
                nc.vector.tensor_scalar(
                    hidden[t][:], mean[:, (t % 2) * V : (t % 2 + 1) * V], unit_sb[:, t : t + 1], None, ALU.mult
                )

        out_rows = out.rearrange("(b p) r -> p b r", p=P)
        label_banks = (2, 3, 5, 6)
        for r in range(U // QUARTER):
            fetched = keep.tile([P, PACK, QUARTER], BF16, name="fetched%d" % r)
            on_vector = 2 - r % 2
            for t in range(PACK):
                window = hidden[t][:].indirect(cell_sb[:, r * (QUARTER // STRIPE) : (r + 1) * (QUARTER // STRIPE)])
                if t < on_vector:
                    nc.vector.tensor_copy(fetched[:, t, :], window)
                else:
                    nc.scalar.activation(fetched[:, t, :], window, ACT.Copy)
            hid = keep.tile([P, QUARTER, PACK], BF16, name="hid%d" % r, align_bytes=64)
            nc.vector.tensor_copy(hid[:], fetched[:].rearrange("p t r -> p r t"))
            hid_codes = keep.tile([P, QUARTER], U32, name="hid_codes%d" % r, align_bytes=64)
            hid_scales = keep.tile([P, QUARTER], U8, name="hid_scales%d" % r, align_bytes=64)
            nc.vector.quantize_mx(
                out=hid_codes[:].bitcast(FP8X4), scales=hid_scales[:], in_=hid[:].rearrange("p r t -> p (r t)")
            )
            labels = bank(label_banks[r], "labels%d" % r)
            for b in range(N // P):
                nc.tensor.matmul_mx(
                    out=labels[:, b * QUARTER : (b + 1) * QUARTER],
                    lhsT=w3_codes[:, b * P : (b + 1) * P].bitcast(FP8X4),
                    lhsT_scale=w3_scales[:, b * P : (b + 1) * P],
                    rhs=hid_codes[:].bitcast(FP8X4),
                    rhs_scale=hid_scales[:],
                    start=True,
                    stop=True,
                )
            staged = keep.tile([P, N // P, QUARTER], F32, name="staged%d" % r)
            nc.scalar.copy(staged[:].rearrange("p b r -> p (b r)"), labels[:, 0 : N // P * QUARTER])
            nc.sync.dma_start(out=out_rows[:, :, r * QUARTER : (r + 1) * QUARTER], in_=staged[:])
